import numpy as np
import ml_dtypes


def mxq(x, axis, fmt="e4m3"):
    dtype, down = {"e4m3": (ml_dtypes.float8_e4m3fn, 7), "e5m2": (ml_dtypes.float8_e5m2, 14)}[fmt]
    v = np.moveaxis(np.asarray(x, np.float32).astype(ml_dtypes.bfloat16).astype(np.float64), axis, -1)
    blocks = v.reshape(v.shape[:-1] + (-1, 32))
    amax = np.abs(blocks).max(-1, keepdims=True)
    byte = np.maximum(np.where(amax > 0, np.frexp(amax)[1] - 1 + 127, 0) - down, 1)
    scale = np.exp2(byte - 127.0)
    codes = (blocks / scale).astype(np.float32).astype(dtype).astype(np.float64)
    return np.moveaxis((codes * scale).reshape(v.shape), -1, axis)


WIDE = False


def mx_kscale(k):
    if not WIDE:
        return np.ones(k)
    levels = np.array([10, -10, 5, -5, 0])
    if k % 512:
        return np.exp2(np.random.permutation(np.resize(levels, k // 32))).repeat(32)
    a = np.empty((k // 512, 16))
    for p in range(k // 512):
        a[p, :8] = np.random.permutation(np.resize(levels, 8))
        for g in range(8):
            far = levels[np.abs(levels - a[p, g]) >= 10]
            a[p, g + 8] = far[np.random.randint(len(far))]
    return np.exp2(a.ravel()).repeat(32)


def f64(x):
    return np.asarray(x).astype(np.float64)


def striped(idx):
    return np.tile(np.asarray(idx).reshape(-1, 16).T, (8, 1)).astype(np.uint16)


def unstriped(offs):
    return offs[:16].T.reshape(-1).astype(np.int64)


def striped8(idx):
    return np.asarray(idx).reshape(8, -1, 16).transpose(0, 2, 1).reshape(128, -1).astype(np.uint16)


def unstriped8(offs):
    return offs.reshape(8, 16, -1).transpose(0, 2, 1).reshape(8, -1).astype(np.int64)


def pick8(x, idx, run):
    r = np.arange(len(x))
    return x[r[:, None], idx[r % (8 * run) // run]]


E2M1 = np.array([0.0, 0.5, 1.0, 1.5, 2.0, 3.0, 4.0, 6.0, -0.0, -0.5, -1.0, -1.5, -2.0, -3.0, -4.0, -6.0])


def pack_weight(w, fmt):
    k, n = w.shape
    w = f64(np.asarray(w, np.float32).astype(ml_dtypes.bfloat16)).reshape(k // 32, 32, n)
    amax = np.abs(w).max(1)
    if fmt == "e4m3":
        byte = np.frexp(amax)[1] - 1 + 127 - 7
    else:
        mant, ex = np.frexp(amax / 6.0)
        byte = np.where(mant > 0.5, ex, ex - 1) + 127
    byte = np.clip(np.where(amax > 0, byte, 1), 1, 254)
    scaled = (w * np.exp2(127.0 - byte)[:, None, :]).reshape(k, n).astype(np.float32)
    by_word = np.ascontiguousarray(scaled.reshape(k // 512, 128, 4, n).transpose(0, 1, 3, 2))
    if fmt == "e4m3":
        words = by_word.astype(ml_dtypes.float8_e4m3fn).view(np.uint8)
    else:
        c = by_word.astype(ml_dtypes.float4_e2m1fn).view(np.uint8) & 0xF
        words = (c[..., 0::2] | (c[..., 1::2] << 4)).reshape(k // 512, 128, 2 * n)
    return np.ascontiguousarray(words), np.ascontiguousarray(byte.astype(np.uint8).reshape(k // 512, 16, n))


def unpack_weight(words, scales, fmt):
    g, _, n = scales.shape
    words = np.ascontiguousarray(words).reshape(g, 128, n, -1)
    if fmt == "e4m3":
        vals = words.view(ml_dtypes.float8_e4m3fn).astype(np.float64)
    else:
        nib = np.empty((g, 128, n, 4), np.uint8)
        nib[..., 0::2] = words & 0xF
        nib[..., 1::2] = words >> 4
        vals = E2M1[nib]
    vals = vals * np.repeat(np.exp2(scales.astype(np.float64) - 127.0), 8, axis=1)[..., None]
    return vals.transpose(0, 1, 3, 2).reshape(g * 512, n)


K, R, F, T, J, U = 512, 128, 512, 2048, 512, 1024


def setup_inputs():
    n = np.random.standard_normal
    idx = np.random.permutation(T)[:J]
    idx2 = np.stack([np.random.permutation(U)[:J] for _ in range(8)])
    fk = mx_kscale(K)
    ff = mx_kscale(F)
    tabp = pack_weight(n((K, T)) / fk[:, None], "e4m3")
    return {
        "tab_words": tabp[0],
        "tab_scales": tabp[1],
        "w1": (n((K, R)) * 1 / np.sqrt(K) * fk[:, None]).astype(np.float32),
        "gain": (np.random.uniform(0.5, 1.5, (R, 1))).astype(np.float32),
        "ground": (n((R, U)) * 0.7).astype(np.float32),
        "wo": (n((F, R)) * 1 / np.sqrt(F) * ff[:, None]).astype(np.float32),
        "dy": (n((F, U)) / ff[:, None]).astype(np.float32),
        "og": (np.random.uniform(0.3, 1.0, (R, 1))).astype(np.float32),
        "base": (0.3 * n((R, J))).astype(np.float32),
        "offs": striped(idx),
        "offs2": striped8(idx2),
    }


def reference(tab_words, tab_scales, w1, gain, ground, wo, dy, og, base, offs, offs2):
    idx = unstriped(offs)
    idx2 = unstriped8(offs2)
    tabu = unpack_weight(tab_words, tab_scales, "e4m3")
    w1q = mxq(f64(w1), 0, "e4m3")
    tabidxg = tabu[:, idx]
    a = w1q.T @ tabidxg
    h1 = a * f64(gain)
    pg = np.zeros((R, U))
    pg[np.arange(R)[:, None], idx2[np.arange(R) % 128 // 16]] = h1
    s = pg + f64(ground)
    u1 = np.tanh(s)
    woq = mxq(f64(wo), 0, "e4m3")
    dyq = mxq(f64(dy), 0, "e4m3")
    c0 = woq.T @ dyq
    ds = c0 * (1.0 - np.square(u1))
    dh1 = pick8(ds, idx2, 16)
    da = dh1 * f64(gain)
    hda = da * 2.0
    hdh1 = hda * f64(gain)
    s51 = np.zeros((R, U))
    s51[np.arange(R)[:, None], idx2[np.arange(R) % 128 // 16]] = hdh1
    hu1 = s51 * c0 * (-1.0) * u1 * 2.0
    hs = hu1 * (1.0 - np.square(u1))
    hh1 = pick8(hs, idx2, 16)
    ha = hh1 * f64(gain)
    y = ha * f64(og) + f64(base)
    return y

@@ -1,0 +1,180 @@
+from contextlib import ExitStack
+
+import concourse.mybir as mybir
+
+K, R, F, T, J, U = 512, 128, 512, 2048, 512, 1024
+FLOPS = 2 * K * R * J + 2 * F * R * U
+
+F32 = mybir.dt.float32
+BF16 = mybir.dt.bfloat16
+I32 = mybir.dt.int32
+U32 = mybir.dt.uint32
+U16 = mybir.dt.uint16
+U8 = mybir.dt.uint8
+FP8X4 = mybir.dt.float8_e4m3fn_x4
+ALU = mybir.AluOpType
+ACT = mybir.ActivationFunctionType
+
+P = 128
+PACK = 4
+HALF = J // 2
+LIST_COLS = HALF // 16
+CHUNK = 256
+N_CHUNKS = U // CHUNK
+
+
+def tile_attend_gppageput_kernel(tc, tab_words, tab_scales, w1, gain, ground, wo, dy, og, base, offs, offs2, out):
+    nc = tc.nc
+
+    def weave_views(grouped, raw):
+        return (
+            grouped[:].rearrange("p (c i) t -> p c t i", i=4),
+            raw[:].rearrange("p t (c i) -> p c t i", i=4),
+        )
+
+    with ExitStack() as ctx:
+        sb = ctx.enter_context(tc.tile_pool(name="sb", bufs=1))
+        ps = ctx.enter_context(tc.psum_pool(name="ps", bufs=1))
+
+        def quantize(grouped, width, name):
+            codes = sb.tile([P, width], U32, name=name + "_codes", align_bytes=64)
+            scales = sb.tile([P, width], U8, name=name + "_scales", align_bytes=64)
+            nc.vector.quantize_mx(
+                out=codes[:].bitcast(FP8X4), scales=scales[:], in_=grouped[:].rearrange("p w t -> p (w t)")
+            )
+            return codes, scales
+
+        tab_bytes = sb.tile([P, T], U8, name="tab_bytes", tag="scale_window", align_bytes=64)
+        nc.vector.memset(tab_bytes[:].bitcast(I32), 0)
+        for q in range(4):
+            nc.scalar.dma_start(
+                out=tab_bytes[32 * q : 32 * q + 4, :].bitcast(I32),
+                in_=tab_scales[0, 4 * q : 4 * q + 4, :].bitcast(I32),
+            )
+        tab_list = sb.tile([P, J // 16], U16, name="tab_list")
+        nc.sync.dma_start(tab_list[:], offs)
+        w1_raw = sb.tile([P, PACK, R], F32, name="w1_raw", align_bytes=64)
+        nc.sync.dma_start(out=w1_raw[:], in_=w1.rearrange("(p t) r -> p t r", t=PACK))
+        tab_codes = sb.tile([P, T], U32, name="tab_codes", align_bytes=64)
+        nc.sync.dma_start(out=tab_codes[:].bitcast(I32), in_=tab_words[0].rearrange("p n t -> p (n t)").bitcast(I32))
+        page_list = sb.tile([P, J // 16], U16, name="page_list")
+        nc.sync.dma_start(page_list[:], offs2)
+        gain_col = sb.tile([P, 1], F32, name="gain_col")
+        nc.scalar.dma_start(out=gain_col[:], in_=gain)
+        og_col = sb.tile([P, 1], F32, name="og_col")
+
+        dy_rows = dy.rearrange("(p t) u -> p t u", t=PACK)
+        dy_raw = [sb.tile([P, PACK, CHUNK], F32, name="dy_raw%d" % c, align_bytes=64) for c in range(N_CHUNKS)]
+        wo_raw = sb.tile([P, PACK, R], F32, name="wo_raw", align_bytes=64)
+        ground_sb = [sb.tile([P, U // 2], F32, name="ground%d" % h, align_bytes=64) for h in range(2)]
+        for c in range(N_CHUNKS):
+            nc.sync.dma_start(out=dy_raw[c][:], in_=dy_rows[:, :, c * CHUNK : (c + 1) * CHUNK])
+            if c == 1:
+                nc.sync.dma_start(out=wo_raw[:], in_=wo.rearrange("(p t) r -> p t r", t=PACK))
+            if c in (1, 2):
+                h = c - 1
+                nc.sync.dma_start(out=ground_sb[h][:], in_=ground[:, h * (U // 2) : (h + 1) * (U // 2)])
+        base_sb = sb.tile([P, J], F32, name="base_sb", align_bytes=64)
+        nc.sync.dma_start(out=og_col[:], in_=og)
+        nc.sync.dma_start(out=base_sb[:], in_=base)
+
+        page = sb.tile([P, U], F32, name="page", align_bytes=64)
+        nc.vector.memset(page[:], 0.0)
+
+        gain_twice = sb.tile([P, 1], F32, name="gain_twice")
+        nc.scalar.activation(gain_twice[:], gain_col[:], ACT.Copy, scale=2.0)
+        put_factor = sb.tile([P, HALF], F32, name="put_factor", align_bytes=64)
+        nc.scalar.activation(put_factor[:], gain_col[:].to_broadcast([P, HALF]), ACT.Copy, scale=gain_twice[:])
+
+        w1_bf = sb.tile([P, R, PACK], BF16, name="w1_bf", align_bytes=64)
+        nc.vector.tensor_copy(*weave_views(w1_bf, w1_raw))
+        w1_codes, w1_scales = quantize(w1_bf, R, "w1")
+        picked_bytes = sb.tile([P, J], U8, name="picked_bytes", align_bytes=64)
+        nc.vector.tensor_copy(picked_bytes[:], tab_bytes[:].indirect(tab_list[:]))
+        halves = [slice(h * HALF, (h + 1) * HALF) for h in range(2)]
+        list_halves = [slice(h * LIST_COLS, (h + 1) * LIST_COLS) for h in range(2)]
+        h1 = []
+        for h in range(2):
+            picked = sb.tile([P, HALF], U32, name="picked%d" % h, tag=("scale_window", "picked1")[h], align_bytes=64)
+            nc.vector.tensor_copy(picked[:], tab_codes[:].indirect(tab_list[:, list_halves[h]]))
+            a_ps = ps.tile([P, HALF], F32, name="a_ps%d" % h)
+            nc.tensor.matmul_mx(
+                out=a_ps[:],
+                lhsT=w1_codes[:].bitcast(FP8X4),
+                lhsT_scale=w1_scales[:],
+                rhs=picked[:].bitcast(FP8X4),
+                rhs_scale=picked_bytes[:, halves[h]],
+                start=True,
+                stop=True,
+            )
+            h1_half = sb.tile([P, HALF], F32, name="h1_%d" % h, align_bytes=64)
+            nc.scalar.activation(h1_half[:], a_ps[:], ACT.Copy, scale=gain_col[:])
+            h1.append(h1_half)
+        for h in range(2):
+            nc.vector.tensor_copy(page[:].indirect(page_list[:, list_halves[h]]), h1[h][:])
+
+        dy_bf = [sb.tile([P, CHUNK, PACK], BF16, name="dy_bf%d" % c, align_bytes=64) for c in range(N_CHUNKS)]
+        wo_bf = sb.tile([P, R, PACK], BF16, name="wo_bf", align_bytes=64)
+        for c in range(N_CHUNKS - 1):
+            dst, src = weave_views(dy_bf[c], dy_raw[c])
+            nc.scalar.activation(dst, src, ACT.Copy)
+            if c == 1:
+                dst, src = weave_views(wo_bf, wo_raw)
+                nc.scalar.activation(dst, src, ACT.Copy, scale=-1.0)
+        dy_q = [quantize(dy_bf[c], CHUNK, "dy%d" % c) for c in range(2)]
+        wo_codes, wo_scales = quantize(wo_bf, R, "wo")
+        nc.vector.tensor_copy(*weave_views(dy_bf[N_CHUNKS - 1], dy_raw[N_CHUNKS - 1]))
+        dy_q = dy_q + [quantize(dy_bf[c], CHUNK, "dy%d" % c) for c in range(2, N_CHUNKS)]
+        neg_c0 = []
+        for c in range(N_CHUNKS):
+            c_ps = ps.tile([P, CHUNK], F32, name="c_ps%d" % c)
+            nc.tensor.matmul_mx(
+                out=c_ps[:],
+                lhsT=wo_codes[:].bitcast(FP8X4),
+                lhsT_scale=wo_scales[:],
+                rhs=dy_q[c][0][:].bitcast(FP8X4),
+                rhs_scale=dy_q[c][1][:],
+                start=True,
+                stop=True,
+            )
+            neg_c0.append(c_ps)
+
+        s = sb.tile([P, U], F32, name="s", align_bytes=64)
+        u1 = sb.tile([P, U], F32, name="u1", align_bytes=64)
+        u1_sq = sb.tile([P, U], F32, name="u1_sq", align_bytes=64)
+        ds = sb.tile([P, U], F32, name="ds", align_bytes=64)
+        chunks = [slice(c * CHUNK, (c + 1) * CHUNK) for c in range(N_CHUNKS)]
+        for c in range(N_CHUNKS):
+            g_cols = slice((c % 2) * CHUNK, (c % 2 + 1) * CHUNK)
+            nc.vector.tensor_tensor(s[:, chunks[c]], page[:, chunks[c]], ground_sb[c // 2][:, g_cols], ALU.add)
+        nc.scalar.activation(u1[:, chunks[0]], s[:, chunks[0]], ACT.Tanh)
+        for c in range(N_CHUNKS):
+            if c + 1 < N_CHUNKS:
+                nc.scalar.activation(u1[:, chunks[c + 1]], s[:, chunks[c + 1]], ACT.Tanh)
+            nc.scalar.activation(u1_sq[:, chunks[c]], u1[:, chunks[c]], ACT.Square)
+        for c in range(N_CHUNKS):
+            nc.vector.scalar_tensor_tensor(
+                ds[:, chunks[c]], u1_sq[:, chunks[c]], 1.0, neg_c0[c][:], ALU.subtract, ALU.mult
+            )
+
+        dh1 = []
+        for h in range(2):
+            dh1_half = sb.tile([P, HALF], F32, name="dh1_%d" % h, align_bytes=64)
+            nc.scalar.activation(dh1_half[:], ds[:].indirect(page_list[:, list_halves[h]]), ACT.Copy)
+            dh1.append(dh1_half)
+        out_factor = sb.tile([P, 1], F32, name="out_factor")
+        nc.scalar.activation(out_factor[:], og_col[:], ACT.Copy, scale=gain_col[:])
+        curve = sb.tile([P, U], F32, name="curve", align_bytes=64)
+        nc.vector.scalar_tensor_tensor(curve[:], u1[:], -2.0, ds[:], ALU.mult, ALU.mult)
+        for h in range(2):
+            nc.vector.tensor_tensor(page[:].indirect(page_list[:, list_halves[h]]), dh1[h][:], put_factor[:], ALU.mult)
+        hs = sb.tile([P, U], F32, name="hs", align_bytes=64)
+        nc.vector.tensor_tensor(hs[:], page[:], curve[:], ALU.mult)
+
+        hh1 = [sb.tile([P, HALF], F32, name="hh1_%d" % h, align_bytes=64) for h in range(2)]
+        nc.scalar.activation(hh1[0][:], hs[:].indirect(page_list[:, list_halves[0]]), ACT.Copy)
+        nc.vector.tensor_copy(hh1[1][:], hs[:].indirect(page_list[:, list_halves[1]]))
+        for h in range(2):
+            y = sb.tile([P, HALF], F32, name="y%d" % h, align_bytes=64)
+            nc.vector.scalar_tensor_tensor(y[:], hh1[h][:], out_factor[:], base_sb[:, halves[h]], ALU.mult, ALU.add)
+            nc.sync.dma_start(out=out[:, halves[h]], in_=y[:])

@@ -21,6 +21,7 @@ HALF = J // 2
 LIST_COLS = HALF // 16
 CHUNK = 256
 N_CHUNKS = U // CHUNK
+VECTOR_COLS = 128
 
 
 def tile_attend_gppageput_kernel(tc, tab_words, tab_scales, w1, gain, ground, wo, dy, og, base, offs, offs2, out):
@@ -28,16 +29,16 @@ def tile_attend_gppageput_kernel(tc, tab_words, tab_scales, w1, gain, ground, wo
 
     def weave_views(grouped, raw):
         return (
-            grouped[:].rearrange("p (c i) t -> p c t i", i=4),
-            raw[:].rearrange("p t (c i) -> p c t i", i=4),
+            grouped.rearrange("p (c i) t -> p c t i", i=4),
+            raw.rearrange("p t (c i) -> p c t i", i=4),
         )
 
     with ExitStack() as ctx:
         sb = ctx.enter_context(tc.tile_pool(name="sb", bufs=1))
         ps = ctx.enter_context(tc.psum_pool(name="ps", bufs=1))
 
-        def quantize(grouped, width, name):
-            codes = sb.tile([P, width], U32, name=name + "_codes", align_bytes=64)
+        def quantize(grouped, width, name, tag=None):
+            codes = sb.tile([P, width], U32, name=name + "_codes", tag=tag or name + "_codes", align_bytes=64)
             scales = sb.tile([P, width], U8, name=name + "_scales", align_bytes=64)
             nc.vector.quantize_mx(
                 out=codes[:].bitcast(FP8X4), scales=scales[:], in_=grouped[:].rearrange("p w t -> p (w t)")
@@ -47,32 +48,35 @@ def tile_attend_gppageput_kernel(tc, tab_words, tab_scales, w1, gain, ground, wo
         tab_bytes = sb.tile([P, T], U8, name="tab_bytes", tag="scale_window", align_bytes=64)
         nc.vector.memset(tab_bytes[:].bitcast(I32), 0)
         for q in range(4):
-            nc.scalar.dma_start(
+            nc.sync.dma_start(
                 out=tab_bytes[32 * q : 32 * q + 4, :].bitcast(I32),
                 in_=tab_scales[0, 4 * q : 4 * q + 4, :].bitcast(I32),
             )
+        tab_codes = sb.tile([P, T], U32, name="tab_codes", align_bytes=64)
+        words = tab_words[0].rearrange("p n t -> p (n t)").bitcast(I32)
+        nc.sync.dma_start(out=tab_codes[:].bitcast(I32)[:, : T // 2], in_=words[:, : T // 2])
         tab_list = sb.tile([P, J // 16], U16, name="tab_list")
         nc.sync.dma_start(tab_list[:], offs)
         w1_raw = sb.tile([P, PACK, R], F32, name="w1_raw", align_bytes=64)
         nc.sync.dma_start(out=w1_raw[:], in_=w1.rearrange("(p t) r -> p t r", t=PACK))
-        tab_codes = sb.tile([P, T], U32, name="tab_codes", align_bytes=64)
-        nc.sync.dma_start(out=tab_codes[:].bitcast(I32), in_=tab_words[0].rearrange("p n t -> p (n t)").bitcast(I32))
+        nc.sync.dma_start(out=tab_codes[:].bitcast(I32)[:, T // 2 :], in_=words[:, T // 2 :])
         page_list = sb.tile([P, J // 16], U16, name="page_list")
         nc.sync.dma_start(page_list[:], offs2)
         gain_col = sb.tile([P, 1], F32, name="gain_col")
-        nc.scalar.dma_start(out=gain_col[:], in_=gain)
+        nc.gpsimd.dma_start(out=gain_col[:], in_=gain)
         og_col = sb.tile([P, 1], F32, name="og_col")
 
         dy_rows = dy.rearrange("(p t) u -> p t u", t=PACK)
-        dy_raw = [sb.tile([P, PACK, CHUNK], F32, name="dy_raw%d" % c, align_bytes=64) for c in range(N_CHUNKS)]
+        dy_raw = [sb.tile([P, PACK, CHUNK], F32, name="dy_raw%d" % c, tag="dy_raw%d" % c, align_bytes=64) for c in range(N_CHUNKS)]
         wo_raw = sb.tile([P, PACK, R], F32, name="wo_raw", align_bytes=64)
-        ground_sb = [sb.tile([P, U // 2], F32, name="ground%d" % h, align_bytes=64) for h in range(2)]
+        ground_sb = [
+            sb.tile([P, U // 2], F32, name="ground%d" % h, tag="ground%d" % h, align_bytes=64) for h in range(2)
+        ]
+        nc.sync.dma_start(out=wo_raw[:], in_=wo.rearrange("(p t) r -> p t r", t=PACK))
         for c in range(N_CHUNKS):
             nc.sync.dma_start(out=dy_raw[c][:], in_=dy_rows[:, :, c * CHUNK : (c + 1) * CHUNK])
-            if c == 1:
-                nc.sync.dma_start(out=wo_raw[:], in_=wo.rearrange("(p t) r -> p t r", t=PACK))
-            if c in (1, 2):
-                h = c - 1
+            if c >= 2:
+                h = c - 2
                 nc.sync.dma_start(out=ground_sb[h][:], in_=ground[:, h * (U // 2) : (h + 1) * (U // 2)])
         base_sb = sb.tile([P, J], F32, name="base_sb", align_bytes=64)
         nc.sync.dma_start(out=og_col[:], in_=og)
@@ -87,8 +91,10 @@ def tile_attend_gppageput_kernel(tc, tab_words, tab_scales, w1, gain, ground, wo
         nc.scalar.activation(put_factor[:], gain_col[:].to_broadcast([P, HALF]), ACT.Copy, scale=gain_twice[:])
 
         w1_bf = sb.tile([P, R, PACK], BF16, name="w1_bf", align_bytes=64)
-        nc.vector.tensor_copy(*weave_views(w1_bf, w1_raw))
+        nc.vector.tensor_copy(*weave_views(w1_bf[:], w1_raw[:]))
         w1_codes, w1_scales = quantize(w1_bf, R, "w1")
+        wo_bf = sb.tile([P, R, PACK], BF16, name="wo_bf", align_bytes=64)
+        nc.scalar.activation(*weave_views(wo_bf[:], wo_raw[:]), ACT.Copy, scale=-1.0)
         picked_bytes = sb.tile([P, J], U8, name="picked_bytes", align_bytes=64)
         nc.vector.tensor_copy(picked_bytes[:], tab_bytes[:].indirect(tab_list[:]))
         halves = [slice(h * HALF, (h + 1) * HALF) for h in range(2)]
@@ -110,58 +116,54 @@ def tile_attend_gppageput_kernel(tc, tab_words, tab_scales, w1, gain, ground, wo
             h1_half = sb.tile([P, HALF], F32, name="h1_%d" % h, align_bytes=64)
             nc.scalar.activation(h1_half[:], a_ps[:], ACT.Copy, scale=gain_col[:])
             h1.append(h1_half)
+        wo_codes, wo_scales = quantize(wo_bf, R, "wo")
         for h in range(2):
             nc.vector.tensor_copy(page[:].indirect(page_list[:, list_halves[h]]), h1[h][:])
 
-        dy_bf = [sb.tile([P, CHUNK, PACK], BF16, name="dy_bf%d" % c, align_bytes=64) for c in range(N_CHUNKS)]
-        wo_bf = sb.tile([P, R, PACK], BF16, name="wo_bf", align_bytes=64)
-        for c in range(N_CHUNKS - 1):
-            dst, src = weave_views(dy_bf[c], dy_raw[c])
-            nc.scalar.activation(dst, src, ACT.Copy)
-            if c == 1:
-                dst, src = weave_views(wo_bf, wo_raw)
-                nc.scalar.activation(dst, src, ACT.Copy, scale=-1.0)
-        dy_q = [quantize(dy_bf[c], CHUNK, "dy%d" % c) for c in range(2)]
-        wo_codes, wo_scales = quantize(wo_bf, R, "wo")
-        nc.vector.tensor_copy(*weave_views(dy_bf[N_CHUNKS - 1], dy_raw[N_CHUNKS - 1]))
-        dy_q = dy_q + [quantize(dy_bf[c], CHUNK, "dy%d" % c) for c in range(2, N_CHUNKS)]
-        neg_c0 = []
+        page_halves = [slice(h * (U // 2), (h + 1) * (U // 2)) for h in range(2)]
+        dy_bf = [
+            sb.tile([P, U // 2, PACK], BF16, name="dy_bf%d" % h, tag=("scale_window", "dy_bf1")[h], align_bytes=64)
+            for h in range(2)
+        ]
         for c in range(N_CHUNKS):
-            c_ps = ps.tile([P, CHUNK], F32, name="c_ps%d" % c)
+            first = VECTOR_COLS if c == 2 else 0
+            cols = slice((c % 2) * CHUNK + first, (c % 2 + 1) * CHUNK)
+            nc.scalar.activation(*weave_views(dy_bf[c // 2][:, cols, :], dy_raw[c][:, :, first:]), ACT.Copy)
+        s = sb.tile([P, U], F32, name="s", align_bytes=64)
+        for h in range(2):
+            nc.vector.tensor_tensor(s[:, page_halves[h]], page[:, page_halves[h]], ground_sb[h][:], ALU.add)
+        nc.vector.tensor_copy(*weave_views(dy_bf[1][:, :VECTOR_COLS, :], dy_raw[2][:, :, :VECTOR_COLS]))
+        neg_c0 = []
+        for h in range(2):
+            dy_codes, dy_scales = quantize(dy_bf[h], U // 2, "dy%d" % h, tag=("ground1", "dy1_codes")[h])
+            c_ps = ps.tile([P, U // 2], F32, name="c_ps%d" % h)
             nc.tensor.matmul_mx(
                 out=c_ps[:],
                 lhsT=wo_codes[:].bitcast(FP8X4),
                 lhsT_scale=wo_scales[:],
-                rhs=dy_q[c][0][:].bitcast(FP8X4),
-                rhs_scale=dy_q[c][1][:],
+                rhs=dy_codes[:].bitcast(FP8X4),
+                rhs_scale=dy_scales[:],
                 start=True,
                 stop=True,
             )
             neg_c0.append(c_ps)
 
-        s = sb.tile([P, U], F32, name="s", align_bytes=64)
-        u1 = sb.tile([P, U], F32, name="u1", align_bytes=64)
+        spans = [slice(0, 2 * CHUNK), slice(2 * CHUNK, 3 * CHUNK), slice(3 * CHUNK, 4 * CHUNK)]
+        c0_spans = [neg_c0[0][:], neg_c0[1][:, 0:CHUNK], neg_c0[1][:, CHUNK : 2 * CHUNK]]
+        u1 = sb.tile([P, U], F32, name="u1", tag="dy_raw3", align_bytes=64)
         u1_sq = sb.tile([P, U], F32, name="u1_sq", align_bytes=64)
-        ds = sb.tile([P, U], F32, name="ds", align_bytes=64)
-        chunks = [slice(c * CHUNK, (c + 1) * CHUNK) for c in range(N_CHUNKS)]
-        for c in range(N_CHUNKS):
-            g_cols = slice((c % 2) * CHUNK, (c % 2 + 1) * CHUNK)
-            nc.vector.tensor_tensor(s[:, chunks[c]], page[:, chunks[c]], ground_sb[c // 2][:, g_cols], ALU.add)
-        nc.scalar.activation(u1[:, chunks[0]], s[:, chunks[0]], ACT.Tanh)
-        for c in range(N_CHUNKS):
-            if c + 1 < N_CHUNKS:
-                nc.scalar.activation(u1[:, chunks[c + 1]], s[:, chunks[c + 1]], ACT.Tanh)
-            nc.scalar.activation(u1_sq[:, chunks[c]], u1[:, chunks[c]], ACT.Square)
-        for c in range(N_CHUNKS):
-            nc.vector.scalar_tensor_tensor(
-                ds[:, chunks[c]], u1_sq[:, chunks[c]], 1.0, neg_c0[c][:], ALU.subtract, ALU.mult
-            )
+        ds = sb.tile([P, U], F32, name="ds", tag="dy_bf1", align_bytes=64)
+        nc.scalar.activation(u1[:, spans[0]], s[:, spans[0]], ACT.Tanh)
+        for i in range(len(spans)):
+            if i + 1 < len(spans):
+                nc.scalar.activation(u1[:, spans[i + 1]], s[:, spans[i + 1]], ACT.Tanh)
+            nc.scalar.activation(u1_sq[:, spans[i]], u1[:, spans[i]], ACT.Square)
+        for i in range(len(spans)):
+            nc.vector.scalar_tensor_tensor(ds[:, spans[i]], u1_sq[:, spans[i]], 1.0, c0_spans[i], ALU.subtract, ALU.mult)
 
-        dh1 = []
+        dh1 = [sb.tile([P, HALF], F32, name="dh1_%d" % h, align_bytes=64) for h in range(2)]
         for h in range(2):
-            dh1_half = sb.tile([P, HALF], F32, name="dh1_%d" % h, align_bytes=64)
-            nc.scalar.activation(dh1_half[:], ds[:].indirect(page_list[:, list_halves[h]]), ACT.Copy)
-            dh1.append(dh1_half)
+            nc.scalar.activation(dh1[h][:], ds[:].indirect(page_list[:, list_halves[h]]), ACT.Copy)
         out_factor = sb.tile([P, 1], F32, name="out_factor")
         nc.scalar.activation(out_factor[:], og_col[:], ACT.Copy, scale=gain_col[:])
         curve = sb.tile([P, U], F32, name="curve", align_bytes=64)

@@ -19,9 +19,10 @@ P = 128
 PACK = 4
 HALF = J // 2
 LIST_COLS = HALF // 16
+FIRST = 128
 CHUNK = 256
 N_CHUNKS = U // CHUNK
-VECTOR_COLS = 128
+VECTOR_COLS = 64
 
 
 def tile_attend_gppageput_kernel(tc, tab_words, tab_scales, w1, gain, ground, wo, dy, og, base, offs, offs2, out):
@@ -63,7 +64,7 @@ def tile_attend_gppageput_kernel(tc, tab_words, tab_scales, w1, gain, ground, wo
         page_list = sb.tile([P, J // 16], U16, name="page_list")
         nc.sync.dma_start(page_list[:], offs2)
         gain_col = sb.tile([P, 1], F32, name="gain_col")
-        nc.gpsimd.dma_start(out=gain_col[:], in_=gain)
+        nc.sync.dma_start(out=gain_col[:], in_=gain)
         og_col = sb.tile([P, 1], F32, name="og_col")
 
         dy_rows = dy.rearrange("(p t) u -> p t u", t=PACK)
@@ -99,26 +100,31 @@ def tile_attend_gppageput_kernel(tc, tab_words, tab_scales, w1, gain, ground, wo
         nc.vector.tensor_copy(picked_bytes[:], tab_bytes[:].indirect(tab_list[:]))
         halves = [slice(h * HALF, (h + 1) * HALF) for h in range(2)]
         list_halves = [slice(h * LIST_COLS, (h + 1) * LIST_COLS) for h in range(2)]
+        pieces = [slice(0, FIRST), slice(FIRST, J)]
+        list_pieces = [slice(sl.start // 16, sl.stop // 16) for sl in pieces]
+        passes = [[slice(0, FIRST)], [slice(0, HALF), slice(HALF, J - FIRST)]]
         h1 = []
-        for h in range(2):
-            picked = sb.tile([P, HALF], U32, name="picked%d" % h, tag=("scale_window", "picked1")[h], align_bytes=64)
-            nc.vector.tensor_copy(picked[:], tab_codes[:].indirect(tab_list[:, list_halves[h]]))
-            a_ps = ps.tile([P, HALF], F32, name="a_ps%d" % h)
-            nc.tensor.matmul_mx(
-                out=a_ps[:],
-                lhsT=w1_codes[:].bitcast(FP8X4),
-                lhsT_scale=w1_scales[:],
-                rhs=picked[:].bitcast(FP8X4),
-                rhs_scale=picked_bytes[:, halves[h]],
-                start=True,
-                stop=True,
-            )
-            h1_half = sb.tile([P, HALF], F32, name="h1_%d" % h, align_bytes=64)
-            nc.scalar.activation(h1_half[:], a_ps[:], ACT.Copy, scale=gain_col[:])
-            h1.append(h1_half)
-        wo_codes, wo_scales = quantize(wo_bf, R, "wo")
-        for h in range(2):
-            nc.vector.tensor_copy(page[:].indirect(page_list[:, list_halves[h]]), h1[h][:])
+        for i in range(2):
+            width = pieces[i].stop - pieces[i].start
+            picked = sb.tile([P, width], U32, name="picked%d" % i, tag=("scale_window", "picked1")[i], align_bytes=64)
+            nc.vector.tensor_copy(picked[:], tab_codes[:].indirect(tab_list[:, list_pieces[i]]))
+            a_ps = ps.tile([P, width], F32, name="a_ps%d" % i)
+            for cols in passes[i]:
+                nc.tensor.matmul_mx(
+                    out=a_ps[:, cols],
+                    lhsT=w1_codes[:].bitcast(FP8X4),
+                    lhsT_scale=w1_scales[:],
+                    rhs=picked[:, cols].bitcast(FP8X4),
+                    rhs_scale=picked_bytes[:, pieces[i]][:, cols],
+                    start=True,
+                    stop=True,
+                )
+            h1_piece = sb.tile([P, width], F32, name="h1_%d" % i, tag="h1_%d" % i, align_bytes=64)
+            nc.scalar.activation(h1_piece[:], a_ps[:], ACT.Copy, scale=gain_col[:])
+            h1.append(h1_piece)
+        nc.vector.tensor_copy(page[:].indirect(page_list[:, list_pieces[0]]), h1[0][:])
+        wo_codes, wo_scales = quantize(wo_bf, R, "wo", tag="h1_0")
+        nc.vector.tensor_copy(page[:].indirect(page_list[:, list_pieces[1]]), h1[1][:])
 
         page_halves = [slice(h * (U // 2), (h + 1) * (U // 2)) for h in range(2)]
         dy_bf = [
@@ -133,25 +139,31 @@ def tile_attend_gppageput_kernel(tc, tab_words, tab_scales, w1, gain, ground, wo
         for h in range(2):
             nc.vector.tensor_tensor(s[:, page_halves[h]], page[:, page_halves[h]], ground_sb[h][:], ALU.add)
         nc.vector.tensor_copy(*weave_views(dy_bf[1][:, :VECTOR_COLS, :], dy_raw[2][:, :, :VECTOR_COLS]))
-        neg_c0 = []
-        for h in range(2):
-            dy_codes, dy_scales = quantize(dy_bf[h], U // 2, "dy%d" % h, tag=("ground1", "dy1_codes")[h])
-            c_ps = ps.tile([P, U // 2], F32, name="c_ps%d" % h)
+        spans = [slice(0, 2 * CHUNK), slice(2 * CHUNK, 3 * CHUNK), slice(3 * CHUNK, 4 * CHUNK)]
+        c0_spans = [ps.tile([P, sp.stop - sp.start], F32, name="c_ps%d" % i) for i, sp in enumerate(spans)]
+        targets = [c0_spans[0][:, :CHUNK], c0_spans[0][:, CHUNK:], c0_spans[1][:], c0_spans[2][:]]
+        dy_codes = sb.tile([P, U], U32, name="dy_codes", tag="ground1", align_bytes=64)
+        dy_scales = sb.tile([P, U], U8, name="dy_scales", align_bytes=64)
+        for c in range(N_CHUNKS):
+            cols = slice(c * CHUNK, (c + 1) * CHUNK)
+            local = slice((c % 2) * CHUNK, (c % 2 + 1) * CHUNK)
+            nc.vector.quantize_mx(
+                out=dy_codes[:, cols].bitcast(FP8X4),
+                scales=dy_scales[:, cols],
+                in_=dy_bf[c // 2][:, local, :].rearrange("p w t -> p (w t)"),
+            )
             nc.tensor.matmul_mx(
-                out=c_ps[:],
+                out=targets[c],
                 lhsT=wo_codes[:].bitcast(FP8X4),
                 lhsT_scale=wo_scales[:],
-                rhs=dy_codes[:].bitcast(FP8X4),
-                rhs_scale=dy_scales[:],
+                rhs=dy_codes[:, cols].bitcast(FP8X4),
+                rhs_scale=dy_scales[:, cols],
                 start=True,
                 stop=True,
             )
-            neg_c0.append(c_ps)
 
-        spans = [slice(0, 2 * CHUNK), slice(2 * CHUNK, 3 * CHUNK), slice(3 * CHUNK, 4 * CHUNK)]
-        c0_spans = [neg_c0[0][:], neg_c0[1][:, 0:CHUNK], neg_c0[1][:, CHUNK : 2 * CHUNK]]
         u1 = sb.tile([P, U], F32, name="u1", tag="dy_raw3", align_bytes=64)
-        u1_sq = sb.tile([P, U], F32, name="u1_sq", align_bytes=64)
+        u1_sq = sb.tile([P, U], F32, name="u1_sq", tag="u1_sq", align_bytes=64)
         ds = sb.tile([P, U], F32, name="ds", tag="dy_bf1", align_bytes=64)
         nc.scalar.activation(u1[:, spans[0]], s[:, spans[0]], ACT.Tanh)
         for i in range(len(spans)):
@@ -159,16 +171,18 @@ def tile_attend_gppageput_kernel(tc, tab_words, tab_scales, w1, gain, ground, wo
                 nc.scalar.activation(u1[:, spans[i + 1]], s[:, spans[i + 1]], ACT.Tanh)
             nc.scalar.activation(u1_sq[:, spans[i]], u1[:, spans[i]], ACT.Square)
         for i in range(len(spans)):
-            nc.vector.scalar_tensor_tensor(ds[:, spans[i]], u1_sq[:, spans[i]], 1.0, c0_spans[i], ALU.subtract, ALU.mult)
+            nc.vector.scalar_tensor_tensor(ds[:, spans[i]], u1_sq[:, spans[i]], 1.0, c0_spans[i][:], ALU.subtract, ALU.mult)
 
         dh1 = [sb.tile([P, HALF], F32, name="dh1_%d" % h, align_bytes=64) for h in range(2)]
         for h in range(2):
             nc.scalar.activation(dh1[h][:], ds[:].indirect(page_list[:, list_halves[h]]), ACT.Copy)
         out_factor = sb.tile([P, 1], F32, name="out_factor")
         nc.scalar.activation(out_factor[:], og_col[:], ACT.Copy, scale=gain_col[:])
-        curve = sb.tile([P, U], F32, name="curve", align_bytes=64)
-        nc.vector.scalar_tensor_tensor(curve[:], u1[:], -2.0, ds[:], ALU.mult, ALU.mult)
+        curve = sb.tile([P, U], F32, name="curve", tag="u1_sq", align_bytes=64)
+        curve_parts = [slice(0, 3 * CHUNK), slice(3 * CHUNK, U)]
         for h in range(2):
+            cols = curve_parts[h]
+            nc.vector.scalar_tensor_tensor(curve[:, cols], u1[:, cols], -2.0, ds[:, cols], ALU.mult, ALU.mult)
             nc.vector.tensor_tensor(page[:].indirect(page_list[:, list_halves[h]]), dh1[h][:], put_factor[:], ALU.mult)
         hs = sb.tile([P, U], F32, name="hs", align_bytes=64)
         nc.vector.tensor_tensor(hs[:], page[:], curve[:], ALU.mult)

from contextlib import ExitStack

import concourse.mybir as mybir

K, R, F, T, J, U = 512, 128, 512, 2048, 512, 1024
FLOPS = 2 * K * R * J + 2 * F * R * U

F32 = mybir.dt.float32
BF16 = mybir.dt.bfloat16
I32 = mybir.dt.int32
U32 = mybir.dt.uint32
U16 = mybir.dt.uint16
U8 = mybir.dt.uint8
FP8X4 = mybir.dt.float8_e4m3fn_x4
ALU = mybir.AluOpType
ACT = mybir.ActivationFunctionType

P = 128
PACK = 4
HALF = J // 2
LIST_COLS = HALF // 16
FIRST = 128
CHUNK = 256
N_CHUNKS = U // CHUNK
VECTOR_COLS = 64


def tile_attend_gppageput_kernel(tc, tab_words, tab_scales, w1, gain, ground, wo, dy, og, base, offs, offs2, out):
    nc = tc.nc

    def weave_views(grouped, raw):
        return (
            grouped.rearrange("p (c i) t -> p c t i", i=4),
            raw.rearrange("p t (c i) -> p c t i", i=4),
        )

    with ExitStack() as ctx:
        sb = ctx.enter_context(tc.tile_pool(name="sb", bufs=1))
        ps = ctx.enter_context(tc.psum_pool(name="ps", bufs=1))

        def quantize(grouped, width, name, tag=None):
            codes = sb.tile([P, width], U32, name=name + "_codes", tag=tag or name + "_codes", align_bytes=64)
            scales = sb.tile([P, width], U8, name=name + "_scales", align_bytes=64)
            nc.vector.quantize_mx(
                out=codes[:].bitcast(FP8X4), scales=scales[:], in_=grouped[:].rearrange("p w t -> p (w t)")
            )
            return codes, scales

        tab_bytes = sb.tile([P, T], U8, name="tab_bytes", tag="scale_window", align_bytes=64)
        nc.vector.memset(tab_bytes[:].bitcast(I32), 0)
        for q in range(4):
            nc.sync.dma_start(
                out=tab_bytes[32 * q : 32 * q + 4, :].bitcast(I32),
                in_=tab_scales[0, 4 * q : 4 * q + 4, :].bitcast(I32),
            )
        tab_codes = sb.tile([P, T], U32, name="tab_codes", align_bytes=64)
        words = tab_words[0].rearrange("p n t -> p (n t)").bitcast(I32)
        nc.sync.dma_start(out=tab_codes[:].bitcast(I32)[:, : T // 2], in_=words[:, : T // 2])
        tab_list = sb.tile([P, J // 16], U16, name="tab_list")
        nc.sync.dma_start(tab_list[:], offs)
        w1_raw = sb.tile([P, PACK, R], F32, name="w1_raw", align_bytes=64)
        nc.sync.dma_start(out=w1_raw[:], in_=w1.rearrange("(p t) r -> p t r", t=PACK))
        nc.sync.dma_start(out=tab_codes[:].bitcast(I32)[:, T // 2 :], in_=words[:, T // 2 :])
        page_list = sb.tile([P, J // 16], U16, name="page_list")
        nc.sync.dma_start(page_list[:], offs2)
        gain_col = sb.tile([P, 1], F32, name="gain_col")
        nc.sync.dma_start(out=gain_col[:], in_=gain)
        og_col = sb.tile([P, 1], F32, name="og_col")

        dy_rows = dy.rearrange("(p t) u -> p t u", t=PACK)
        dy_raw = [sb.tile([P, PACK, CHUNK], F32, name="dy_raw%d" % c, tag="dy_raw%d" % c, align_bytes=64) for c in range(N_CHUNKS)]
        wo_raw = sb.tile([P, PACK, R], F32, name="wo_raw", align_bytes=64)
        ground_sb = [
            sb.tile([P, U // 2], F32, name="ground%d" % h, tag="ground%d" % h, align_bytes=64) for h in range(2)
        ]
        nc.sync.dma_start(out=wo_raw[:], in_=wo.rearrange("(p t) r -> p t r", t=PACK))
        for c in range(N_CHUNKS):
            nc.sync.dma_start(out=dy_raw[c][:], in_=dy_rows[:, :, c * CHUNK : (c + 1) * CHUNK])
            if c >= 2:
                h = c - 2
                nc.sync.dma_start(out=ground_sb[h][:], in_=ground[:, h * (U // 2) : (h + 1) * (U // 2)])
        base_sb = sb.tile([P, J], F32, name="base_sb", align_bytes=64)
        nc.sync.dma_start(out=og_col[:], in_=og)
        nc.sync.dma_start(out=base_sb[:], in_=base)

        page = sb.tile([P, U], F32, name="page", align_bytes=64)
        nc.vector.memset(page[:], 0.0)

        gain_twice = sb.tile([P, 1], F32, name="gain_twice")
        nc.scalar.activation(gain_twice[:], gain_col[:], ACT.Copy, scale=2.0)
        put_factor = sb.tile([P, HALF], F32, name="put_factor", align_bytes=64)
        nc.scalar.activation(put_factor[:], gain_col[:].to_broadcast([P, HALF]), ACT.Copy, scale=gain_twice[:])

        w1_bf = sb.tile([P, R, PACK], BF16, name="w1_bf", align_bytes=64)
        nc.vector.tensor_copy(*weave_views(w1_bf[:], w1_raw[:]))
        w1_codes, w1_scales = quantize(w1_bf, R, "w1")
        wo_bf = sb.tile([P, R, PACK], BF16, name="wo_bf", align_bytes=64)
        nc.scalar.activation(*weave_views(wo_bf[:], wo_raw[:]), ACT.Copy, scale=-1.0)
        picked_bytes = sb.tile([P, J], U8, name="picked_bytes", align_bytes=64)
        nc.vector.tensor_copy(picked_bytes[:], tab_bytes[:].indirect(tab_list[:]))
        halves = [slice(h * HALF, (h + 1) * HALF) for h in range(2)]
        list_halves = [slice(h * LIST_COLS, (h + 1) * LIST_COLS) for h in range(2)]
        pieces = [slice(0, FIRST), slice(FIRST, J)]
        list_pieces = [slice(sl.start // 16, sl.stop // 16) for sl in pieces]
        passes = [[slice(0, FIRST)], [slice(0, HALF), slice(HALF, J - FIRST)]]
        h1 = []
        for i in range(2):
            width = pieces[i].stop - pieces[i].start
            picked = sb.tile([P, width], U32, name="picked%d" % i, tag=("scale_window", "picked1")[i], align_bytes=64)
            nc.vector.tensor_copy(picked[:], tab_codes[:].indirect(tab_list[:, list_pieces[i]]))
            a_ps = ps.tile([P, width], F32, name="a_ps%d" % i)
            for cols in passes[i]:
                nc.tensor.matmul_mx(
                    out=a_ps[:, cols],
                    lhsT=w1_codes[:].bitcast(FP8X4),
                    lhsT_scale=w1_scales[:],
                    rhs=picked[:, cols].bitcast(FP8X4),
                    rhs_scale=picked_bytes[:, pieces[i]][:, cols],
                    start=True,
                    stop=True,
                )
            h1_piece = sb.tile([P, width], F32, name="h1_%d" % i, tag="h1_%d" % i, align_bytes=64)
            nc.scalar.activation(h1_piece[:], a_ps[:], ACT.Copy, scale=gain_col[:])
            h1.append(h1_piece)
        nc.vector.tensor_copy(page[:].indirect(page_list[:, list_pieces[0]]), h1[0][:])
        wo_codes, wo_scales = quantize(wo_bf, R, "wo", tag="h1_0")
        nc.vector.tensor_copy(page[:].indirect(page_list[:, list_pieces[1]]), h1[1][:])

        page_halves = [slice(h * (U // 2), (h + 1) * (U // 2)) for h in range(2)]
        dy_bf = [
            sb.tile([P, U // 2, PACK], BF16, name="dy_bf%d" % h, tag=("scale_window", "dy_bf1")[h], align_bytes=64)
            for h in range(2)
        ]
        for c in range(N_CHUNKS):
            first = VECTOR_COLS if c == 2 else 0
            cols = slice((c % 2) * CHUNK + first, (c % 2 + 1) * CHUNK)
            nc.scalar.activation(*weave_views(dy_bf[c // 2][:, cols, :], dy_raw[c][:, :, first:]), ACT.Copy)
        s = sb.tile([P, U], F32, name="s", align_bytes=64)
        for h in range(2):
            nc.vector.tensor_tensor(s[:, page_halves[h]], page[:, page_halves[h]], ground_sb[h][:], ALU.add)
        nc.vector.tensor_copy(*weave_views(dy_bf[1][:, :VECTOR_COLS, :], dy_raw[2][:, :, :VECTOR_COLS]))
        spans = [slice(0, 2 * CHUNK), slice(2 * CHUNK, 3 * CHUNK), slice(3 * CHUNK, 4 * CHUNK)]
        c0_spans = [ps.tile([P, sp.stop - sp.start], F32, name="c_ps%d" % i) for i, sp in enumerate(spans)]
        targets = [c0_spans[0][:, :CHUNK], c0_spans[0][:, CHUNK:], c0_spans[1][:], c0_spans[2][:]]
        dy_codes = sb.tile([P, U], U32, name="dy_codes", tag="ground1", align_bytes=64)
        dy_scales = sb.tile([P, U], U8, name="dy_scales", align_bytes=64)
        for c in range(N_CHUNKS):
            cols = slice(c * CHUNK, (c + 1) * CHUNK)
            local = slice((c % 2) * CHUNK, (c % 2 + 1) * CHUNK)
            nc.vector.quantize_mx(
                out=dy_codes[:, cols].bitcast(FP8X4),
                scales=dy_scales[:, cols],
                in_=dy_bf[c // 2][:, local, :].rearrange("p w t -> p (w t)"),
            )
            nc.tensor.matmul_mx(
                out=targets[c],
                lhsT=wo_codes[:].bitcast(FP8X4),
                lhsT_scale=wo_scales[:],
                rhs=dy_codes[:, cols].bitcast(FP8X4),
                rhs_scale=dy_scales[:, cols],
                start=True,
                stop=True,
            )

        u1 = sb.tile([P, U], F32, name="u1", tag="dy_raw3", align_bytes=64)
        u1_sq = sb.tile([P, U], F32, name="u1_sq", tag="u1_sq", align_bytes=64)
        ds = sb.tile([P, U], F32, name="ds", tag="dy_bf1", align_bytes=64)
        nc.scalar.activation(u1[:, spans[0]], s[:, spans[0]], ACT.Tanh)
        for i in range(len(spans)):
            if i + 1 < len(spans):
                nc.scalar.activation(u1[:, spans[i + 1]], s[:, spans[i + 1]], ACT.Tanh)
            nc.scalar.activation(u1_sq[:, spans[i]], u1[:, spans[i]], ACT.Square)
        for i in range(len(spans)):
            nc.vector.scalar_tensor_tensor(ds[:, spans[i]], u1_sq[:, spans[i]], 1.0, c0_spans[i][:], ALU.subtract, ALU.mult)

        dh1 = [sb.tile([P, HALF], F32, name="dh1_%d" % h, align_bytes=64) for h in range(2)]
        for h in range(2):
            nc.scalar.activation(dh1[h][:], ds[:].indirect(page_list[:, list_halves[h]]), ACT.Copy)
        out_factor = sb.tile([P, 1], F32, name="out_factor")
        nc.scalar.activation(out_factor[:], og_col[:], ACT.Copy, scale=gain_col[:])
        curve = sb.tile([P, U], F32, name="curve", tag="u1_sq", align_bytes=64)
        curve_parts = [slice(0, 3 * CHUNK), slice(3 * CHUNK, U)]
        for h in range(2):
            cols = curve_parts[h]
            nc.vector.scalar_tensor_tensor(curve[:, cols], u1[:, cols], -2.0, ds[:, cols], ALU.mult, ALU.mult)
            nc.vector.tensor_tensor(page[:].indirect(page_list[:, list_halves[h]]), dh1[h][:], put_factor[:], ALU.mult)
        hs = sb.tile([P, U], F32, name="hs", align_bytes=64)
        nc.vector.tensor_tensor(hs[:], page[:], curve[:], ALU.mult)

        hh1 = [sb.tile([P, HALF], F32, name="hh1_%d" % h, align_bytes=64) for h in range(2)]
        nc.scalar.activation(hh1[0][:], hs[:].indirect(page_list[:, list_halves[0]]), ACT.Copy)
        nc.vector.tensor_copy(hh1[1][:], hs[:].indirect(page_list[:, list_halves[1]]))
        for h in range(2):
            y = sb.tile([P, HALF], F32, name="y%d" % h, align_bytes=64)
            nc.vector.scalar_tensor_tensor(y[:], hh1[h][:], out_factor[:], base_sb[:, halves[h]], ALU.mult, ALU.add)
            nc.sync.dma_start(out=out[:, halves[h]], in_=y[:])
